import numpy as np
import ml_dtypes


def mxq(x, axis, fmt="e4m3"):
    dtype, down = {"e4m3": (ml_dtypes.float8_e4m3fn, 7), "e5m2": (ml_dtypes.float8_e5m2, 14)}[fmt]
    v = np.moveaxis(np.asarray(x, np.float32).astype(ml_dtypes.bfloat16).astype(np.float64), axis, -1)
    blocks = v.reshape(v.shape[:-1] + (-1, 32))
    amax = np.abs(blocks).max(-1, keepdims=True)
    byte = np.maximum(np.where(amax > 0, np.frexp(amax)[1] - 1 + 127, 0) - down, 1)
    scale = np.exp2(byte - 127.0)
    codes = (blocks / scale).astype(np.float32).astype(dtype).astype(np.float64)
    return np.moveaxis((codes * scale).reshape(v.shape), -1, axis)


WIDE = False


def mx_kscale(k):
    if not WIDE:
        return np.ones(k)
    levels = np.array([10, -10, 5, -5, 0])
    if k % 512:
        return np.exp2(np.random.permutation(np.resize(levels, k // 32))).repeat(32)
    a = np.empty((k // 512, 16))
    for p in range(k // 512):
        a[p, :8] = np.random.permutation(np.resize(levels, 8))
        for g in range(8):
            far = levels[np.abs(levels - a[p, g]) >= 10]
            a[p, g + 8] = far[np.random.randint(len(far))]
    return np.exp2(a.ravel()).repeat(32)


def f64(x):
    return np.asarray(x).astype(np.float64)


def striped8(idx):
    return np.concatenate([x.reshape(-1, 16).T for x in idx]).astype(np.uint16)


def runs(offs, k):
    lists = np.stack([offs[16 * r : 16 * r + 16].T.reshape(-1) for r in range(8)]).astype(np.int64)
    return lists[np.arange(k) % 512 // 64]


def pack_weight(w):
    k, n = w.shape
    w = f64(np.asarray(w, np.float32).astype(ml_dtypes.bfloat16)).reshape(k // 32, 32, n)
    amax = np.abs(w).max(1)
    byte = np.clip(np.where(amax > 0, np.frexp(amax)[1] - 1 + 127 - 7, 1), 1, 254)
    scaled = (w * np.exp2(127.0 - byte)[:, None, :]).reshape(k, n).astype(np.float32)
    words = np.ascontiguousarray(scaled.reshape(k // 512, 128, 4, n).transpose(0, 1, 3, 2)).astype(ml_dtypes.float8_e4m3fn).view(np.uint8)
    return words, np.ascontiguousarray(byte.astype(np.uint8).reshape(k // 512, 16, n))


def unpack_weight(words, scales):
    g, p, n, _ = words.shape
    vals = np.ascontiguousarray(words).view(ml_dtypes.float8_e4m3fn).astype(np.float64) * np.repeat(np.exp2(scales.astype(np.float64) - 127.0), 8, axis=1)[..., None]
    return vals.transpose(0, 1, 3, 2).reshape(g * 512, n)


K, T, S, H, G, W = 512, 2048, 512, 512, 2048, 256


def setup_inputs():
    n = np.random.standard_normal
    s = mx_kscale(K)[:, None]
    packed_xT = pack_weight(n((K, T)) * s)
    packed_dT = pack_weight(n((K, G)) / s)
    perm = np.stack([np.random.permutation(S) for _ in range(8)])
    return {
        "x_words": packed_xT[0],
        "x_scales": packed_xT[1],
        "w1": (n((K, H)) / np.sqrt(K) / s).astype(np.float32),
        "gs": (np.random.uniform(0.5, 1.5, (K, 1)) * s).astype(np.float32),
        "d_words": packed_dT[0],
        "d_scales": packed_dT[1],
        "offs": striped8(np.random.randint(0, T, (8, S))),
        "k1": striped8(np.random.randint(0, G, (8, H))),
        "n1": striped8(perm[:, :W]),
        "n2": striped8(perm[:, W:]),
        "n3": striped8(np.stack([np.random.permutation(S) for _ in range(8)])),
    }


def reference(x_words, x_scales, w1, gs, d_words, d_scales, offs, k1, n1, n2, n3):
    d_k1 = unpack_weight(d_words, d_scales)[np.arange(K)[:, None], runs(k1, K)]
    xq = unpack_weight(x_words, x_scales)[np.arange(K)[:, None], runs(offs, K)]
    y = mxq(f64(w1), 0, "e4m3").T @ xq
    z = f64(gs) * y
    h = 0.0625 * ((d_k1.T @ mxq(z, 0, "e4m3")))
    pa = h[np.arange(H)[:, None], runs(n1, H)]
    pb = h[np.arange(H)[:, None], runs(n2, H)]
    rb = pa - pb
    ra = pa + pb
    ds = np.zeros((H, S))
    ds[np.arange(H)[:, None], runs(n1, H)] = ra
    dt = ds.copy()
    dt[np.arange(H)[:, None], runs(n2, H)] = rb
    return np.maximum(dt, dt[np.arange(H)[:, None], runs(n3, H)])

@@ -1,0 +1,184 @@
+from contextlib import ExitStack
+
+import concourse.mybir as mybir
+
+K, T, S, H, G, W = 512, 2048, 512, 512, 2048, 256
+FLOPS = 2 * K * H * S + 2 * H * H * S
+
+F32 = mybir.dt.float32
+BF16 = mybir.dt.bfloat16
+I32 = mybir.dt.int32
+U32 = mybir.dt.uint32
+U16 = mybir.dt.uint16
+U8 = mybir.dt.uint8
+FP8X4 = mybir.dt.float8_e4m3fn_x4
+ALU = mybir.AluOpType
+ACT = mybir.ActivationFunctionType
+
+P = 128
+PACK = 4
+GROUP = 16
+QUAD = 32
+CHUNK = 128
+W1_PARTS = 2
+
+
+def tile_picked_hdenseihaarh_none_p_kernel(
+    tc, x_words, x_scales, w1, gs, d_words, d_scales, offs, k1, n1, n2, n3, out
+):
+    nc = tc.nc
+    with ExitStack() as ctx:
+        keep = ctx.enter_context(tc.tile_pool(name="keep", bufs=1))
+        psum = ctx.enter_context(tc.psum_pool(name="psum", bufs=1))
+
+        def sb(name, shape, dtype):
+            return keep.tile(shape, dtype, name=name, align_bytes=64)
+
+        def load_list(name, src):
+            tile = keep.tile(list(src.shape), U16, name=name)
+            nc.sync.dma_start(tile[:], src)
+            return tile
+
+        def load_scale_table(name, src):
+            tile = sb(name, [P, src.shape[2]], U8)
+            nc.vector.memset(tile[:].bitcast(I32), 0)
+            nc.gpsimd.dma_start(tile[0:P:8, :].bitcast(I32), src[0].bitcast(I32))
+            return tile
+
+        def load_word_table(name, src):
+            tile = sb(name, [P, src.shape[2]], U32)
+            nc.sync.dma_start(tile[:].bitcast(I32), src[0].rearrange("p n r -> p (n r)").bitcast(I32))
+            return tile
+
+        def place_scale_rows(name, picked):
+            plane = sb(name, [P, S], U8)
+            nc.vector.tensor_copy(plane[:].bitcast(I32), picked[:].bitcast(I32))
+            for e in range(1, 4):
+                nc.scalar.dma_start(plane[e:P:QUAD, :].bitcast(I32), picked[8 * e : P : QUAD, :].bitcast(I32))
+            return plane
+
+        offs_sb = load_list("offs_sb", offs)
+        k1_sb = load_list("k1_sb", k1)
+        xs_table = load_scale_table("xs_table", x_scales)
+        ds_table = load_scale_table("ds_table", d_scales)
+        gs_sb = sb("gs_sb", [P, PACK], F32)
+        nc.gpsimd.dma_start(gs_sb[:], gs.rearrange("(p t) o -> p (t o)", t=PACK))
+
+        w1_cols = H // W1_PARTS
+        w1_raw = []
+        for u in range(W1_PARTS):
+            raw = sb(f"w1_raw{u}", [P, PACK, w1_cols], F32)
+            nc.sync.dma_start(raw[:], w1.rearrange("(p j) c -> p j c", j=PACK)[:, :, u * w1_cols : (u + 1) * w1_cols])
+            w1_raw.append(raw)
+        xw_table = load_word_table("xw_table", x_words)
+        dw_table = load_word_table("dw_table", d_words)
+        n1_sb = load_list("n1_sb", n1)
+        n2_sb = load_list("n2_sb", n2)
+        n3_sb = load_list("n3_sb", n3)
+
+        xs_picked = sb("xs_picked", [P, S], U8)
+        nc.vector.tensor_copy(xs_picked[:], xs_table[:].indirect(offs_sb[:]))
+        xs_plane = place_scale_rows("xs_plane", xs_picked)
+        ds_picked = sb("ds_picked", [P, H], U8)
+        nc.vector.tensor_copy(ds_picked[:], ds_table[:].indirect(k1_sb[:]))
+        ds_dealt = sb("ds_dealt", [P, H], U8)
+        nc.vector.tensor_copy(
+            ds_dealt[:].rearrange("p (t m) -> p m t", t=PACK), ds_picked[:].rearrange("p (m t) -> p m t", t=PACK)
+        )
+        ds_plane = place_scale_rows("ds_plane", ds_dealt)
+
+        w1_bf = sb("w1_bf", [P, PACK * H], BF16)
+        w1_view = w1_bf[:].rearrange("p (t m j) -> p m j t", t=PACK, j=PACK)
+        m_part = w1_cols // PACK
+        for u in range(W1_PARTS):
+            nc.scalar.copy(
+                w1_view[:, u * m_part : (u + 1) * m_part], w1_raw[u][:].rearrange("p j (m t) -> p m j t", t=PACK)
+            )
+        w1_codes = sb("w1_codes", [P, H], U32)
+        w1_plane = sb("w1_plane", [P, H], U8)
+        nc.vector.quantize_mx(out=w1_codes[:].bitcast(FP8X4), scales=w1_plane[:], in_=w1_bf[:])
+
+        xw_picked = sb("xw_picked", [P, S], U32)
+        z_codes = sb("z_codes", [P, S], U32)
+        z_plane = sb("z_plane", [P, S], U8)
+        half = S // 2
+        for u in range(2):
+            nc.vector.tensor_copy(
+                xw_picked[:, u * half : (u + 1) * half],
+                xw_table[:].indirect(offs_sb[:, u * half // 16 : (u + 1) * half // 16]),
+            )
+        gs_wide = gs_sb[:].unsqueeze(1).to_broadcast([P, CHUNK, PACK])
+        z_bf = []
+        for c in range(S // CHUNK):
+            cols = slice(c * CHUNK, (c + 1) * CHUNK)
+            y_bank = psum.tile([P, PACK, CHUNK], F32, name=f"y_bank{c}")
+            for t in range(PACK):
+                rows = slice(t * P, (t + 1) * P)
+                nc.tensor.matmul_mx(
+                    out=y_bank[:, t, :],
+                    lhsT=w1_codes[:, rows].bitcast(FP8X4),
+                    lhsT_scale=w1_plane[:, rows],
+                    rhs=xw_picked[:, cols].bitcast(FP8X4),
+                    rhs_scale=xs_plane[:, cols],
+                    start=True,
+                    stop=True,
+                )
+            zc = sb(f"z_bf{c}", [P, CHUNK * PACK], BF16)
+            nc.vector.tensor_tensor(
+                zc[:].rearrange("p (n t) -> p n t", t=PACK), y_bank[:].rearrange("p t n -> p n t"), gs_wide, ALU.mult
+            )
+            z_bf.append(zc)
+            if c > 0:
+                prev = slice((c - 1) * CHUNK, c * CHUNK)
+                nc.vector.quantize_mx(out=z_codes[:, prev].bitcast(FP8X4), scales=z_plane[:, prev], in_=z_bf[c - 1][:])
+
+        dw_picked = sb("dw_picked", [P, H], U32)
+        nc.vector.tensor_copy(dw_picked[:], dw_table[:].indirect(k1_sb[:]))
+        last = slice(S - CHUNK, S)
+        nc.vector.quantize_mx(out=z_codes[:, last].bitcast(FP8X4), scales=z_plane[:, last], in_=z_bf[-1][:])
+        dw_dealt = sb("dw_dealt", [P, H], U32)
+        nc.vector.tensor_copy(
+            dw_dealt[:].rearrange("p (t m) -> p m t", t=PACK), dw_picked[:].rearrange("p (m t) -> p m t", t=PACK)
+        )
+
+        out_rows = out.rearrange("(p t) j -> p t j", t=PACK)
+        for t in range(PACK):
+            rows = slice(t * P, (t + 1) * P)
+            h_bank = psum.tile([P, S], F32, name=f"h_bank{t}")
+            nc.tensor.matmul_mx(
+                out=h_bank[:],
+                lhsT=dw_dealt[:, rows].bitcast(FP8X4),
+                lhsT_scale=ds_plane[:, rows],
+                rhs=z_codes[:].bitcast(FP8X4),
+                rhs_scale=z_plane[:],
+                start=True,
+                stop=True,
+            )
+            h = sb(f"h{t}", [P, S], F32)
+            nc.scalar.activation(h[:], h_bank[:], ACT.Copy, scale=0.0625)
+            pa = sb(f"pa{t}", [P, W], F32)
+            pb = sb(f"pb{t}", [P, W], F32)
+            nc.scalar.activation(pa[:], h[:].indirect(n1_sb[:]), ACT.Copy)
+            if t == 0:
+                nc.vector.tensor_copy(pb[:], h[:].indirect(n2_sb[:]))
+            else:
+                nc.scalar.activation(pb[:], h[:].indirect(n2_sb[:]), ACT.Copy)
+            dt = sb(f"dt{t}", [P, S], F32)
+            nc.vector.tensor_tensor(dt[:].indirect(n1_sb[:]), pa[:], pb[:], ALU.add)
+            pb_neg = sb(f"pb_neg{t}", [P, W], F32)
+            nc.scalar.activation(pb_neg[:], pb[:], ACT.Copy, scale=-1.0)
+            nc.vector.tensor_tensor(dt[:].indirect(n2_sb[:]), pa[:], pb_neg[:], ALU.add)
+            other = sb(f"other{t}", [P, S], F32)
+            for u in range(2):
+                nc.scalar.activation(
+                    other[:, u * half : (u + 1) * half],
+                    dt[:].indirect(n3_sb[:, u * half // 16 : (u + 1) * half // 16]),
+                    ACT.Copy,
+                )
+            res = sb(f"res{t}", [P, S], F32)
+            pieces = 2 if t == PACK - 1 else 1
+            width = S // pieces
+            for u in range(pieces):
+                cols = slice(u * width, (u + 1) * width)
+                nc.vector.tensor_tensor(res[:, cols], dt[:, cols], other[:, cols], ALU.max)
+                nc.sync.dma_start(out_rows[:, t, cols], res[:, cols])

@@ -21,6 +21,7 @@ GROUP = 16
 QUAD = 32
 CHUNK = 128
 W1_PARTS = 2
+W1_SCALAR_LAST = 40
 
 
 def tile_picked_hdenseihaarh_none_p_kernel(
@@ -31,22 +32,26 @@ def tile_picked_hdenseihaarh_none_p_kernel(
         keep = ctx.enter_context(tc.tile_pool(name="keep", bufs=1))
         psum = ctx.enter_context(tc.psum_pool(name="psum", bufs=1))
 
-        def sb(name, shape, dtype):
-            return keep.tile(shape, dtype, name=name, align_bytes=64)
+        reuse = ctx.enter_context(tc.tile_pool(name="reuse", bufs=1))
+
+        def sb(name, shape, dtype, tag=None):
+            if isinstance(tag, int):
+                return reuse.tile(shape, dtype, name=name, offset=tag, align_bytes=64)
+            return keep.tile(shape, dtype, name=name, tag=tag or name, align_bytes=64)
 
         def load_list(name, src):
             tile = keep.tile(list(src.shape), U16, name=name)
             nc.sync.dma_start(tile[:], src)
             return tile
 
-        def load_scale_table(name, src):
-            tile = sb(name, [P, src.shape[2]], U8)
+        def load_scale_table(name, src, tag=None):
+            tile = sb(name, [P, src.shape[2]], U8, tag)
             nc.vector.memset(tile[:].bitcast(I32), 0)
-            nc.gpsimd.dma_start(tile[0:P:8, :].bitcast(I32), src[0].bitcast(I32))
+            nc.sync.dma_start(tile[0:P:8, :].bitcast(I32), src[0].bitcast(I32))
             return tile
 
-        def load_word_table(name, src):
-            tile = sb(name, [P, src.shape[2]], U32)
+        def load_word_table(name, src, tag=None):
+            tile = sb(name, [P, src.shape[2]], U32, tag)
             nc.sync.dma_start(tile[:].bitcast(I32), src[0].rearrange("p n r -> p (n r)").bitcast(I32))
             return tile
 
@@ -54,108 +59,158 @@ def tile_picked_hdenseihaarh_none_p_kernel(
             plane = sb(name, [P, S], U8)
             nc.vector.tensor_copy(plane[:].bitcast(I32), picked[:].bitcast(I32))
             for e in range(1, 4):
-                nc.scalar.dma_start(plane[e:P:QUAD, :].bitcast(I32), picked[8 * e : P : QUAD, :].bitcast(I32))
+                nc.sync.dma_start(plane[e:P:QUAD, :].bitcast(I32), picked[8 * e : P : QUAD, :].bitcast(I32))
             return plane
 
         offs_sb = load_list("offs_sb", offs)
         k1_sb = load_list("k1_sb", k1)
-        xs_table = load_scale_table("xs_table", x_scales)
-        ds_table = load_scale_table("ds_table", d_scales)
         gs_sb = sb("gs_sb", [P, PACK], F32)
-        nc.gpsimd.dma_start(gs_sb[:], gs.rearrange("(p t) o -> p (t o)", t=PACK))
-
+        nc.sync.dma_start(gs_sb[:], gs.rearrange("(p t) o -> p (t o)", t=PACK))
+        n1_sb = load_list("n1_sb", n1)
         w1_cols = H // W1_PARTS
-        w1_raw = []
-        for u in range(W1_PARTS):
+
+        def load_w1(u):
             raw = sb(f"w1_raw{u}", [P, PACK, w1_cols], F32)
             nc.sync.dma_start(raw[:], w1.rearrange("(p j) c -> p j c", j=PACK)[:, :, u * w1_cols : (u + 1) * w1_cols])
-            w1_raw.append(raw)
-        xw_table = load_word_table("xw_table", x_words)
-        dw_table = load_word_table("dw_table", d_words)
-        n1_sb = load_list("n1_sb", n1)
+            return raw
+
+        xs_table = load_scale_table("xs_table", x_scales, 0)
+        w1_raw = [load_w1(0)]
+        ds_table = load_scale_table("ds_table", d_scales)
+        w1_raw.append(load_w1(1))
+        xw_table = load_word_table("xw_table", x_words, "shared_codes")
         n2_sb = load_list("n2_sb", n2)
         n3_sb = load_list("n3_sb", n3)
+        xs_plane = sb("xs_plane", [P, S], U8)
+        nc.vector.memset(xs_plane[:].bitcast(I32), 0)
 
         xs_picked = sb("xs_picked", [P, S], U8)
         nc.vector.tensor_copy(xs_picked[:], xs_table[:].indirect(offs_sb[:]))
-        xs_plane = place_scale_rows("xs_plane", xs_picked)
+        for e in range(4):
+            nc.sync.dma_start(xs_plane[e:P:QUAD, :].bitcast(I32), xs_picked[8 * e : P : QUAD, :].bitcast(I32))
+        dw_table = load_word_table("dw_table", d_words, 0)
         ds_picked = sb("ds_picked", [P, H], U8)
         nc.vector.tensor_copy(ds_picked[:], ds_table[:].indirect(k1_sb[:]))
+
         ds_dealt = sb("ds_dealt", [P, H], U8)
         nc.vector.tensor_copy(
-            ds_dealt[:].rearrange("p (t m) -> p m t", t=PACK), ds_picked[:].rearrange("p (m t) -> p m t", t=PACK)
+            ds_dealt[:].rearrange("p (t b i) -> p b t i", t=PACK, i=16),
+            ds_picked[:].rearrange("p (b i t) -> p b t i", t=PACK, i=16),
         )
         ds_plane = place_scale_rows("ds_plane", ds_dealt)
 
-        w1_bf = sb("w1_bf", [P, PACK * H], BF16)
+
+        w1_bf = sb("w1_bf", [P, PACK * H], BF16, "shared_w1")
         w1_view = w1_bf[:].rearrange("p (t m j) -> p m j t", t=PACK, j=PACK)
         m_part = w1_cols // PACK
         for u in range(W1_PARTS):
-            nc.scalar.copy(
-                w1_view[:, u * m_part : (u + 1) * m_part], w1_raw[u][:].rearrange("p j (m t) -> p m j t", t=PACK)
-            )
+            raw_view = w1_raw[u][:].rearrange("p j (m t) -> p m j t", t=PACK)
+            split = m_part if u < W1_PARTS - 1 else W1_SCALAR_LAST
+            nc.scalar.copy(w1_view[:, u * m_part : u * m_part + split], raw_view[:, :split])
+            if split < m_part:
+                nc.vector.tensor_copy(w1_view[:, u * m_part + split : (u + 1) * m_part], raw_view[:, split:])
         w1_codes = sb("w1_codes", [P, H], U32)
         w1_plane = sb("w1_plane", [P, H], U8)
         nc.vector.quantize_mx(out=w1_codes[:].bitcast(FP8X4), scales=w1_plane[:], in_=w1_bf[:])
 
-        xw_picked = sb("xw_picked", [P, S], U32)
-        z_codes = sb("z_codes", [P, S], U32)
-        z_plane = sb("z_plane", [P, S], U8)
+        xw_picked = sb("xw_picked", [P, S], U32, "shared_w1")
         half = S // 2
         for u in range(2):
             nc.vector.tensor_copy(
                 xw_picked[:, u * half : (u + 1) * half],
                 xw_table[:].indirect(offs_sb[:, u * half // 16 : (u + 1) * half // 16]),
             )
-        gs_wide = gs_sb[:].unsqueeze(1).to_broadcast([P, CHUNK, PACK])
-        z_bf = []
-        for c in range(S // CHUNK):
-            cols = slice(c * CHUNK, (c + 1) * CHUNK)
-            y_bank = psum.tile([P, PACK, CHUNK], F32, name=f"y_bank{c}")
-            for t in range(PACK):
-                rows = slice(t * P, (t + 1) * P)
-                nc.tensor.matmul_mx(
-                    out=y_bank[:, t, :],
-                    lhsT=w1_codes[:, rows].bitcast(FP8X4),
-                    lhsT_scale=w1_plane[:, rows],
-                    rhs=xw_picked[:, cols].bitcast(FP8X4),
-                    rhs_scale=xs_plane[:, cols],
-                    start=True,
-                    stop=True,
-                )
-            zc = sb(f"z_bf{c}", [P, CHUNK * PACK], BF16)
-            nc.vector.tensor_tensor(
-                zc[:].rearrange("p (n t) -> p n t", t=PACK), y_bank[:].rearrange("p t n -> p n t"), gs_wide, ALU.mult
-            )
-            z_bf.append(zc)
-            if c > 0:
-                prev = slice((c - 1) * CHUNK, c * CHUNK)
-                nc.vector.quantize_mx(out=z_codes[:, prev].bitcast(FP8X4), scales=z_plane[:, prev], in_=z_bf[c - 1][:])
-
-        dw_picked = sb("dw_picked", [P, H], U32)
-        nc.vector.tensor_copy(dw_picked[:], dw_table[:].indirect(k1_sb[:]))
-        last = slice(S - CHUNK, S)
-        nc.vector.quantize_mx(out=z_codes[:, last].bitcast(FP8X4), scales=z_plane[:, last], in_=z_bf[-1][:])
-        dw_dealt = sb("dw_dealt", [P, H], U32)
-        nc.vector.tensor_copy(
-            dw_dealt[:].rearrange("p (t m) -> p m t", t=PACK), dw_picked[:].rearrange("p (m t) -> p m t", t=PACK)
-        )
-
-        out_rows = out.rearrange("(p t) j -> p t j", t=PACK)
-        for t in range(PACK):
+        def first_product(bank_slice, t, cols):
             rows = slice(t * P, (t + 1) * P)
-            h_bank = psum.tile([P, S], F32, name=f"h_bank{t}")
             nc.tensor.matmul_mx(
-                out=h_bank[:],
-                lhsT=dw_dealt[:, rows].bitcast(FP8X4),
-                lhsT_scale=ds_plane[:, rows],
-                rhs=z_codes[:].bitcast(FP8X4),
-                rhs_scale=z_plane[:],
+                out=bank_slice,
+                lhsT=w1_codes[:, rows].bitcast(FP8X4),
+                lhsT_scale=w1_plane[:, rows],
+                rhs=xw_picked[:, cols].bitcast(FP8X4),
+                rhs_scale=xs_plane[:, cols],
                 start=True,
                 stop=True,
             )
-            h = sb(f"h{t}", [P, S], F32)
-            nc.scalar.activation(h[:], h_bank[:], ACT.Copy, scale=0.0625)
+
+        def quantize_z(u, c, src):
+            cols = slice(c * CHUNK, (c + 1) * CHUNK)
+            nc.vector.quantize_mx(out=z_codes[u][:, cols].bitcast(FP8X4), scales=z_plane[u][:, cols], in_=src[:])
+
+        def scale_on_vector(c, gains, tag):
+            y_bank = psum.tile([P, PACK, CHUNK], F32, name=f"y_bank{c}", tag=f"bank{c}")
+            for t in range(PACK):
+                first_product(y_bank[:, t, :], t, slice(c * CHUNK, (c + 1) * CHUNK))
+            zc = sb(f"z_bf{c}", [P, CHUNK * PACK], BF16, tag)
+            nc.vector.tensor_tensor(
+                zc[:].rearrange("p (n t) -> p n t", t=PACK),
+                y_bank[:].rearrange("p t n -> p n t"),
+                gains[:].unsqueeze(1).to_broadcast([P, CHUNK, PACK]),
+                ALU.mult,
+            )
+            return zc
+
+        z_plane = [sb(f"z_plane{u}", [P, half], U8) for u in range(2)]
+        z_codes = [sb("z_codes0", [P, half], U32)]
+        z_bf0 = scale_on_vector(0, gs_sb, None)
+        z_rows = sb("z_rows", [P, PACK, half], BF16)
+        for pair in range(2):
+            y_bank = psum.tile([P, 2, half], F32, name=f"y_pair{pair}", tag=f"bank{2 + pair}")
+            for e in range(2):
+                first_product(y_bank[:, e, :], 2 * pair + e, slice(half, S))
+            for e in range(2):
+                t = 2 * pair + e
+                nc.scalar.activation(z_rows[:, t, :], y_bank[:, e, :], ACT.Copy, scale=gs_sb[:, t : t + 1])
+        z_late = []
+        for c in range(half // CHUNK):
+            zc = sb(f"z_late{c}", [P, CHUNK * PACK], BF16)
+            nc.scalar.copy(
+                zc[:].rearrange("p (n t) -> p n t", t=PACK),
+                z_rows[:, :, c * CHUNK : (c + 1) * CHUNK].rearrange("p t n -> p n t"),
+            )
+            z_late.append(zc)
+        dw_picked = sb("dw_picked", [P, H], U32, "shared_codes")
+        nc.vector.tensor_copy(dw_picked[:], dw_table[:].indirect(k1_sb[:]))
+        quantize_z(0, 0, z_bf0)
+        dw_dealt = sb("dw_dealt", [P, H], U32)
+        nc.vector.tensor_copy(
+            dw_dealt[:].rearrange("p (t b i) -> p b t i", t=PACK, i=4),
+            dw_picked[:].rearrange("p (b i t) -> p b t i", t=PACK, i=4),
+        )
+        quantize_z(0, 1, scale_on_vector(1, gs_sb, 0))
+        z_codes.append(sb("z_codes1", [P, half], U32, 4096))
+        for c in range(half // CHUNK):
+            quantize_z(1, c, z_late[c])
+
+        out_rows = out.rearrange("(p t) j -> p t j", t=PACK)
+        pas, pbs, dts = [], [], []
+
+        def second_product(bank_slice, t, u, cols):
+            nc.tensor.matmul_mx(
+                out=bank_slice,
+                lhsT=dw_dealt[:, t * P : (t + 1) * P].bitcast(FP8X4),
+                lhsT_scale=ds_plane[:, t * P : (t + 1) * P],
+                rhs=z_codes[u][:, cols].bitcast(FP8X4),
+                rhs_scale=z_plane[u][:, cols],
+                start=True,
+                stop=True,
+            )
+
+        def product_and_pairs(t):
+            h = sb(f"h{t}", [P, S], F32, (None, 8192, 9216, 9216)[t])
+            if t < 2:
+                for u in range(2):
+                    bank = psum.tile([P, half], F32, name=f"h_half{t}{u}", tag=f"bank{4 + 2 * t + u}")
+                    second_product(bank[:], t, u, slice(0, half))
+                    cols = slice(u * half, (u + 1) * half)
+                    if (t, u) == (0, 1):
+                        nc.vector.tensor_scalar(h[:, cols], bank[:], 0.0625, None, ALU.mult)
+                    else:
+                        nc.scalar.activation(h[:, cols], bank[:], ACT.Copy, scale=0.0625)
+            else:
+                bank = psum.tile([P, S], F32, name=f"h_bank{t}", tag=f"bank{1 + 2 * t}")
+                for u in range(2):
+                    second_product(bank[:, u * half : (u + 1) * half], t, u, slice(0, half))
+                nc.scalar.activation(h[:], bank[:], ACT.Copy, scale=0.0625)
             pa = sb(f"pa{t}", [P, W], F32)
             pb = sb(f"pb{t}", [P, W], F32)
             nc.scalar.activation(pa[:], h[:].indirect(n1_sb[:]), ACT.Copy)
@@ -165,9 +220,17 @@ def tile_picked_hdenseihaarh_none_p_kernel(
                 nc.scalar.activation(pb[:], h[:].indirect(n2_sb[:]), ACT.Copy)
             dt = sb(f"dt{t}", [P, S], F32)
             nc.vector.tensor_tensor(dt[:].indirect(n1_sb[:]), pa[:], pb[:], ALU.add)
-            pb_neg = sb(f"pb_neg{t}", [P, W], F32)
-            nc.scalar.activation(pb_neg[:], pb[:], ACT.Copy, scale=-1.0)
-            nc.vector.tensor_tensor(dt[:].indirect(n2_sb[:]), pa[:], pb_neg[:], ALU.add)
+            pas.append(pa)
+            pbs.append(pb)
+            dts.append(dt)
+
+        def differences(t):
+            pb_neg = sb(f"pb_neg{t}", [P, W], F32, 8192 if t == 0 else None)
+            nc.scalar.activation(pb_neg[:], pbs[t][:], ACT.Copy, scale=-1.0)
+            nc.vector.tensor_tensor(dts[t][:].indirect(n2_sb[:]), pas[t][:], pb_neg[:], ALU.add)
+
+        def larger_and_store(t):
+            dt = dts[t]
             other = sb(f"other{t}", [P, S], F32)
             for u in range(2):
                 nc.scalar.activation(
@@ -182,3 +245,11 @@ def tile_picked_hdenseihaarh_none_p_kernel(
                 cols = slice(u * width, (u + 1) * width)
                 nc.vector.tensor_tensor(res[:, cols], dt[:, cols], other[:, cols], ALU.max)
                 nc.sync.dma_start(out_rows[:, t, cols], res[:, cols])
+
+        for step in range(PACK + 3):
+            if step < PACK:
+                product_and_pairs(step)
+            if 1 <= step <= PACK:
+                differences(step - 1)
+            if step >= 3:
+                larger_and_store(step - 3)

from contextlib import ExitStack

import concourse.mybir as mybir

K, T, S, H, G, W = 512, 2048, 512, 512, 2048, 256
FLOPS = 2 * K * H * S + 2 * H * H * S

F32 = mybir.dt.float32
BF16 = mybir.dt.bfloat16
I32 = mybir.dt.int32
U32 = mybir.dt.uint32
U16 = mybir.dt.uint16
U8 = mybir.dt.uint8
FP8X4 = mybir.dt.float8_e4m3fn_x4
ALU = mybir.AluOpType
ACT = mybir.ActivationFunctionType

P = 128
PACK = 4
GROUP = 16
QUAD = 32
CHUNK = 128
W1_PARTS = 2
W1_SCALAR_LAST = 40


def tile_picked_hdenseihaarh_none_p_kernel(
    tc, x_words, x_scales, w1, gs, d_words, d_scales, offs, k1, n1, n2, n3, out
):
    nc = tc.nc
    with ExitStack() as ctx:
        keep = ctx.enter_context(tc.tile_pool(name="keep", bufs=1))
        psum = ctx.enter_context(tc.psum_pool(name="psum", bufs=1))

        reuse = ctx.enter_context(tc.tile_pool(name="reuse", bufs=1))

        def sb(name, shape, dtype, tag=None):
            if isinstance(tag, int):
                return reuse.tile(shape, dtype, name=name, offset=tag, align_bytes=64)
            return keep.tile(shape, dtype, name=name, tag=tag or name, align_bytes=64)

        def load_list(name, src):
            tile = keep.tile(list(src.shape), U16, name=name)
            nc.sync.dma_start(tile[:], src)
            return tile

        def load_scale_table(name, src, tag=None):
            tile = sb(name, [P, src.shape[2]], U8, tag)
            nc.vector.memset(tile[:].bitcast(I32), 0)
            nc.sync.dma_start(tile[0:P:8, :].bitcast(I32), src[0].bitcast(I32))
            return tile

        def load_word_table(name, src, tag=None):
            tile = sb(name, [P, src.shape[2]], U32, tag)
            nc.sync.dma_start(tile[:].bitcast(I32), src[0].rearrange("p n r -> p (n r)").bitcast(I32))
            return tile

        def place_scale_rows(name, picked):
            plane = sb(name, [P, S], U8)
            nc.vector.tensor_copy(plane[:].bitcast(I32), picked[:].bitcast(I32))
            for e in range(1, 4):
                nc.sync.dma_start(plane[e:P:QUAD, :].bitcast(I32), picked[8 * e : P : QUAD, :].bitcast(I32))
            return plane

        offs_sb = load_list("offs_sb", offs)
        k1_sb = load_list("k1_sb", k1)
        gs_sb = sb("gs_sb", [P, PACK], F32)
        nc.sync.dma_start(gs_sb[:], gs.rearrange("(p t) o -> p (t o)", t=PACK))
        n1_sb = load_list("n1_sb", n1)
        w1_cols = H // W1_PARTS

        def load_w1(u):
            raw = sb(f"w1_raw{u}", [P, PACK, w1_cols], F32)
            nc.sync.dma_start(raw[:], w1.rearrange("(p j) c -> p j c", j=PACK)[:, :, u * w1_cols : (u + 1) * w1_cols])
            return raw

        xs_table = load_scale_table("xs_table", x_scales, 0)
        w1_raw = [load_w1(0)]
        ds_table = load_scale_table("ds_table", d_scales)
        w1_raw.append(load_w1(1))
        xw_table = load_word_table("xw_table", x_words, "shared_codes")
        n2_sb = load_list("n2_sb", n2)
        n3_sb = load_list("n3_sb", n3)
        xs_plane = sb("xs_plane", [P, S], U8)
        nc.vector.memset(xs_plane[:].bitcast(I32), 0)

        xs_picked = sb("xs_picked", [P, S], U8)
        nc.vector.tensor_copy(xs_picked[:], xs_table[:].indirect(offs_sb[:]))
        for e in range(4):
            nc.sync.dma_start(xs_plane[e:P:QUAD, :].bitcast(I32), xs_picked[8 * e : P : QUAD, :].bitcast(I32))
        dw_table = load_word_table("dw_table", d_words, 0)
        ds_picked = sb("ds_picked", [P, H], U8)
        nc.vector.tensor_copy(ds_picked[:], ds_table[:].indirect(k1_sb[:]))

        ds_dealt = sb("ds_dealt", [P, H], U8)
        nc.vector.tensor_copy(
            ds_dealt[:].rearrange("p (t b i) -> p b t i", t=PACK, i=16),
            ds_picked[:].rearrange("p (b i t) -> p b t i", t=PACK, i=16),
        )
        ds_plane = place_scale_rows("ds_plane", ds_dealt)


        w1_bf = sb("w1_bf", [P, PACK * H], BF16, "shared_w1")
        w1_view = w1_bf[:].rearrange("p (t m j) -> p m j t", t=PACK, j=PACK)
        m_part = w1_cols // PACK
        for u in range(W1_PARTS):
            raw_view = w1_raw[u][:].rearrange("p j (m t) -> p m j t", t=PACK)
            split = m_part if u < W1_PARTS - 1 else W1_SCALAR_LAST
            nc.scalar.copy(w1_view[:, u * m_part : u * m_part + split], raw_view[:, :split])
            if split < m_part:
                nc.vector.tensor_copy(w1_view[:, u * m_part + split : (u + 1) * m_part], raw_view[:, split:])
        w1_codes = sb("w1_codes", [P, H], U32)
        w1_plane = sb("w1_plane", [P, H], U8)
        nc.vector.quantize_mx(out=w1_codes[:].bitcast(FP8X4), scales=w1_plane[:], in_=w1_bf[:])

        xw_picked = sb("xw_picked", [P, S], U32, "shared_w1")
        half = S // 2
        for u in range(2):
            nc.vector.tensor_copy(
                xw_picked[:, u * half : (u + 1) * half],
                xw_table[:].indirect(offs_sb[:, u * half // 16 : (u + 1) * half // 16]),
            )
        def first_product(bank_slice, t, cols):
            rows = slice(t * P, (t + 1) * P)
            nc.tensor.matmul_mx(
                out=bank_slice,
                lhsT=w1_codes[:, rows].bitcast(FP8X4),
                lhsT_scale=w1_plane[:, rows],
                rhs=xw_picked[:, cols].bitcast(FP8X4),
                rhs_scale=xs_plane[:, cols],
                start=True,
                stop=True,
            )

        def quantize_z(u, c, src):
            cols = slice(c * CHUNK, (c + 1) * CHUNK)
            nc.vector.quantize_mx(out=z_codes[u][:, cols].bitcast(FP8X4), scales=z_plane[u][:, cols], in_=src[:])

        def scale_on_vector(c, gains, tag):
            y_bank = psum.tile([P, PACK, CHUNK], F32, name=f"y_bank{c}", tag=f"bank{c}")
            for t in range(PACK):
                first_product(y_bank[:, t, :], t, slice(c * CHUNK, (c + 1) * CHUNK))
            zc = sb(f"z_bf{c}", [P, CHUNK * PACK], BF16, tag)
            nc.vector.tensor_tensor(
                zc[:].rearrange("p (n t) -> p n t", t=PACK),
                y_bank[:].rearrange("p t n -> p n t"),
                gains[:].unsqueeze(1).to_broadcast([P, CHUNK, PACK]),
                ALU.mult,
            )
            return zc

        z_plane = [sb(f"z_plane{u}", [P, half], U8) for u in range(2)]
        z_codes = [sb("z_codes0", [P, half], U32)]
        z_bf0 = scale_on_vector(0, gs_sb, None)
        z_rows = sb("z_rows", [P, PACK, half], BF16)
        for pair in range(2):
            y_bank = psum.tile([P, 2, half], F32, name=f"y_pair{pair}", tag=f"bank{2 + pair}")
            for e in range(2):
                first_product(y_bank[:, e, :], 2 * pair + e, slice(half, S))
            for e in range(2):
                t = 2 * pair + e
                nc.scalar.activation(z_rows[:, t, :], y_bank[:, e, :], ACT.Copy, scale=gs_sb[:, t : t + 1])
        z_late = []
        for c in range(half // CHUNK):
            zc = sb(f"z_late{c}", [P, CHUNK * PACK], BF16)
            nc.scalar.copy(
                zc[:].rearrange("p (n t) -> p n t", t=PACK),
                z_rows[:, :, c * CHUNK : (c + 1) * CHUNK].rearrange("p t n -> p n t"),
            )
            z_late.append(zc)
        dw_picked = sb("dw_picked", [P, H], U32, "shared_codes")
        nc.vector.tensor_copy(dw_picked[:], dw_table[:].indirect(k1_sb[:]))
        quantize_z(0, 0, z_bf0)
        dw_dealt = sb("dw_dealt", [P, H], U32)
        nc.vector.tensor_copy(
            dw_dealt[:].rearrange("p (t b i) -> p b t i", t=PACK, i=4),
            dw_picked[:].rearrange("p (b i t) -> p b t i", t=PACK, i=4),
        )
        quantize_z(0, 1, scale_on_vector(1, gs_sb, 0))
        z_codes.append(sb("z_codes1", [P, half], U32, 4096))
        for c in range(half // CHUNK):
            quantize_z(1, c, z_late[c])

        out_rows = out.rearrange("(p t) j -> p t j", t=PACK)
        pas, pbs, dts = [], [], []

        def second_product(bank_slice, t, u, cols):
            nc.tensor.matmul_mx(
                out=bank_slice,
                lhsT=dw_dealt[:, t * P : (t + 1) * P].bitcast(FP8X4),
                lhsT_scale=ds_plane[:, t * P : (t + 1) * P],
                rhs=z_codes[u][:, cols].bitcast(FP8X4),
                rhs_scale=z_plane[u][:, cols],
                start=True,
                stop=True,
            )

        def product_and_pairs(t):
            h = sb(f"h{t}", [P, S], F32, (None, 8192, 9216, 9216)[t])
            if t < 2:
                for u in range(2):
                    bank = psum.tile([P, half], F32, name=f"h_half{t}{u}", tag=f"bank{4 + 2 * t + u}")
                    second_product(bank[:], t, u, slice(0, half))
                    cols = slice(u * half, (u + 1) * half)
                    if (t, u) == (0, 1):
                        nc.vector.tensor_scalar(h[:, cols], bank[:], 0.0625, None, ALU.mult)
                    else:
                        nc.scalar.activation(h[:, cols], bank[:], ACT.Copy, scale=0.0625)
            else:
                bank = psum.tile([P, S], F32, name=f"h_bank{t}", tag=f"bank{1 + 2 * t}")
                for u in range(2):
                    second_product(bank[:, u * half : (u + 1) * half], t, u, slice(0, half))
                nc.scalar.activation(h[:], bank[:], ACT.Copy, scale=0.0625)
            pa = sb(f"pa{t}", [P, W], F32)
            pb = sb(f"pb{t}", [P, W], F32)
            nc.scalar.activation(pa[:], h[:].indirect(n1_sb[:]), ACT.Copy)
            if t == 0:
                nc.vector.tensor_copy(pb[:], h[:].indirect(n2_sb[:]))
            else:
                nc.scalar.activation(pb[:], h[:].indirect(n2_sb[:]), ACT.Copy)
            dt = sb(f"dt{t}", [P, S], F32)
            nc.vector.tensor_tensor(dt[:].indirect(n1_sb[:]), pa[:], pb[:], ALU.add)
            pas.append(pa)
            pbs.append(pb)
            dts.append(dt)

        def differences(t):
            pb_neg = sb(f"pb_neg{t}", [P, W], F32, 8192 if t == 0 else None)
            nc.scalar.activation(pb_neg[:], pbs[t][:], ACT.Copy, scale=-1.0)
            nc.vector.tensor_tensor(dts[t][:].indirect(n2_sb[:]), pas[t][:], pb_neg[:], ALU.add)

        def larger_and_store(t):
            dt = dts[t]
            other = sb(f"other{t}", [P, S], F32)
            for u in range(2):
                nc.scalar.activation(
                    other[:, u * half : (u + 1) * half],
                    dt[:].indirect(n3_sb[:, u * half // 16 : (u + 1) * half // 16]),
                    ACT.Copy,
                )
            res = sb(f"res{t}", [P, S], F32)
            pieces = 2 if t == PACK - 1 else 1
            width = S // pieces
            for u in range(pieces):
                cols = slice(u * width, (u + 1) * width)
                nc.vector.tensor_tensor(res[:, cols], dt[:, cols], other[:, cols], ALU.max)
                nc.sync.dma_start(out_rows[:, t, cols], res[:, cols])

        for step in range(PACK + 3):
            if step < PACK:
                product_and_pairs(step)
            if 1 <= step <= PACK:
                differences(step - 1)
            if step >= 3:
                larger_and_store(step - 3)
